import numpy as np
import ml_dtypes


def mxq(x, axis, fmt="e4m3"):
    dtype, down = {"e4m3": (ml_dtypes.float8_e4m3fn, 7), "e5m2": (ml_dtypes.float8_e5m2, 14)}[fmt]
    v = np.moveaxis(np.asarray(x, np.float32).astype(ml_dtypes.bfloat16).astype(np.float64), axis, -1)
    blocks = v.reshape(v.shape[:-1] + (-1, 32))
    amax = np.abs(blocks).max(-1, keepdims=True)
    byte = np.maximum(np.where(amax > 0, np.frexp(amax)[1] - 1 + 127, 0) - down, 1)
    scale = np.exp2(byte - 127.0)
    codes = (blocks / scale).astype(np.float32).astype(dtype).astype(np.float64)
    return np.moveaxis((codes * scale).reshape(v.shape), -1, axis)


WIDE = False


def mx_kscale(k):
    if not WIDE:
        return np.ones(k)
    levels = np.array([30, -30])
    if k % 512:
        return np.exp2(np.random.permutation(np.resize(levels, k // 32))).repeat(32)
    a = np.empty((k // 512, 16))
    for p in range(k // 512):
        a[p, :8] = np.random.permutation(np.resize(levels, 8))
        for g in range(8):
            far = levels[np.abs(levels - a[p, g]) >= 10]
            a[p, g + 8] = far[np.random.randint(len(far))]
    return np.exp2(a.ravel()).repeat(32)


BF16 = ml_dtypes.bfloat16


def bf(x):
    return np.asarray(x, np.float32).astype(BF16)


def f64(x):
    return np.asarray(x).astype(np.float64)


T, L, D = 1536, 2048, 1024


def setup_inputs():
    s = mx_kscale(L)
    t = mx_kscale(D)
    loud = np.random.standard_normal((D, T)) * np.exp(0.8 * np.random.standard_normal((D, T)))
    return {"frames": bf(np.random.standard_normal((T, L)) * s),
            "filters": bf(np.random.standard_normal((D, L)) / np.sqrt(L) / s),
            "echo": bf(loud * t[:, None]),
            "decay": bf(np.random.uniform(0.5, 0.95, D)),
            "mixer": bf(np.random.standard_normal((D, D)) / np.sqrt(D) / t),
            "bias": bf(0.3 * np.random.standard_normal(D)),
            "gain": bf(np.random.uniform(0.5, 1.5, T))}


def reference(frames, filters, echo, decay, mixer, bias, gain):
    fq = mxq(f64(filters), 1, "e4m3")
    xq = mxq(f64(frames), 1, "e4m3")
    bands = fq @ xq.T
    damped = f64(echo) * f64(decay)[:, None]
    mq = mxq(f64(mixer), 1, "e4m3")
    eq = mxq(damped, 0, "e5m2")
    mixed = mq @ eq
    z = bands + mixed + f64(bias)[:, None]
    return np.maximum(z, 0.0) * f64(gain)[None, :]

@@ -1,0 +1,258 @@
+from contextlib import ExitStack
+
+import concourse.mybir as mybir
+from concourse.masks import make_identity
+
+T, L, D = 1536, 2048, 1024
+FLOPS = 2 * D * T * (L + D)
+
+F32 = mybir.dt.float32
+BF16 = mybir.dt.bfloat16
+U32 = mybir.dt.uint32
+U8 = mybir.dt.uint8
+E4M3X4 = mybir.dt.float8_e4m3fn_x4
+E5M2X4 = mybir.dt.float8_e5m2_x4
+ACT = mybir.ActivationFunctionType
+ALU = mybir.AluOpType
+
+P = 128
+PACK = 4
+K_PASS = P * PACK
+N = 512
+SLABS = 4
+BAND_TILES = D // P
+BANK_PASSES = L // K_PASS
+MIX_PASSES = D // K_PASS
+PASSES = BANK_PASSES + MIX_PASSES
+BANKS = 8
+FIRST_SORTED_STEP = 6
+FIRST_GAIN_STEP = 10
+GAINS_PER_SLOT = 1
+ACT_WEAVES = ()
+SORT_EARLY = ()
+LATE_GAINS = 2
+ECHO_AFTER = 3
+
+
+def tile_filter_bank_mixer_s2_kernel(tc, frames, filters, echo, decay, mixer, bias, gain, out):
+    nc = tc.nc
+    filter_rows = filters.rearrange("(p m) k -> p m k", m=BAND_TILES)
+    mixer_rows = mixer.rearrange("(p m) k -> p m k", m=BAND_TILES)
+    out_rows = out.rearrange("(p m) t -> p m t", m=BAND_TILES)
+    frame_rows = frames.rearrange("(n c p) k -> n p c k", c=SLABS, p=P)
+    echo_rows = echo.rearrange("(e p j) t -> e p j t", p=P, j=PACK)
+
+    with ExitStack() as ctx:
+        keep = ctx.enter_context(tc.tile_pool(name="keep", bufs=1))
+        work = ctx.enter_context(tc.tile_pool(name="work", bufs=1))
+        psum = ctx.enter_context(tc.psum_pool(name="psum", bufs=1))
+        ctx.enter_context(tc.manual_schedule())
+
+        raw = {}
+        sorted_words = {}
+        woven = {}
+        damped = {}
+        codes = {}
+        scales = {}
+        sums = {}
+        done = {}
+        rectified = []
+        free_banks = list(range(BANKS))
+
+        def load(src, keys):
+            width = len(keys) * K_PASS
+            if len(keys) == 1:
+                tile = work.tile([P, SLABS * width], BF16, name="single", tag="single", bufs=10, align_bytes=64)
+            else:
+                tile = work.tile([P, SLABS * width], BF16, name="double", tag="double", bufs=8, align_bytes=64)
+            nc.sync.dma_start(out=tile[:].rearrange("p (c k) -> p c k", c=SLABS), in_=src)
+            for i, key in enumerate(keys):
+                raw[key] = (tile, i, len(keys))
+
+        def load_frames(n, g, count):
+            load(frame_rows[n][:, :, g * K_PASS:(g + count) * K_PASS], [("frames", n, g + i) for i in range(count)])
+
+        def load_weights(h, g, count):
+            rows, g0 = (filter_rows, g) if g < BANK_PASSES else (mixer_rows, g - BANK_PASSES)
+            load(rows[:, SLABS * h:SLABS * (h + 1), g0 * K_PASS:(g0 + count) * K_PASS],
+                 [("weights", h, g + i) for i in range(count)])
+
+        def load_echo(n, g, count):
+            load(echo_rows[g - BANK_PASSES][:, :, n * N:(n + count) * N], [("echo", n + i, g) for i in range(count)])
+
+        def raw_words(key):
+            tile, i, count = raw[key]
+            half = K_PASS // 2
+            return tile[:].bitcast(F32).rearrange("p (c w) -> p c w", c=SLABS)[:, :, i * half:(i + 1) * half]
+
+        def take_bank():
+            b = free_banks.pop(0)
+            bank = psum.tile([P, N], F32, name="bank%d" % b, tag="bank%d" % b)
+            return b, bank
+
+        def sort_words(key):
+            tile = work.tile([P, SLABS * 2 * P], F32, name="sorted", tag="sorted", bufs=3, align_bytes=64)
+            nc.vector.tensor_copy(out=tile[:].rearrange("p (c u w) -> p c u w", c=SLABS, u=2),
+                                  in_=raw_words(key).rearrange("p c (w u) -> p c u w", u=2))
+            sorted_words[key] = tile
+
+        def new_woven(key):
+            tile = work.tile([P, N * PACK], BF16, name="woven", tag="woven", bufs=5, align_bytes=64)
+            woven[key] = tile
+            return tile
+
+        def turn(key, split=False):
+            if key in sorted_words:
+                src = sorted_words[key][:].rearrange("p (c u w) -> p c u w", c=SLABS, u=2)
+            else:
+                src = raw_words(key).rearrange("p c (w u) -> p c u w", u=2)
+            dst = new_woven(key)[:].bitcast(F32)
+            for pair in range(SLABS // 2):
+                b, bank = take_bank()
+                for c in range(2):
+                    for u in range(2):
+                        j = 2 * c + u
+                        nc.tensor.transpose(bank[:, j * P:(j + 1) * P], src[:, 2 * pair + c, u, :], identity[:])
+                copy = nc.vector.tensor_copy if split and pair == 1 else nc.scalar.copy
+                copy(out=dst[:, pair * N:(pair + 1) * N].rearrange("p (c r u) -> p c r u", c=2, u=2),
+                     in_=bank[:].rearrange("p (c u r) -> p c r u", c=2, u=2))
+                free_banks.append(b)
+
+        def quantize(key):
+            side = "stationary" if key[0] == "weights" else "moving"
+            codes[key] = keep.tile([P, N], U32, name="codes_%s%d%d" % key, tag="codes_" + side, bufs=2 * PASSES, align_bytes=64)
+            scales[key] = keep.tile([P, N], U8, name="scales_%s%d%d" % key, tag="scales_" + side, bufs=2 * PASSES, align_bytes=64)
+            fmt = E5M2X4 if key[0] == "echo" else E4M3X4
+            nc.vector.quantize_mx(out=codes[key][:].bitcast(fmt), scales=scales[key][:], in_=woven[key][:])
+
+        def damp(key):
+            tile, i, count = raw[key]
+            src = tile[:].rearrange("p (j t) -> p j t", j=PACK)
+            dst = work.tile([P, PACK * N], BF16, name="damped", tag="damped", bufs=2, align_bytes=64)
+            for j in range(PACK):
+                col = (key[2] - BANK_PASSES) * PACK + j
+                nc.vector.tensor_scalar(out=dst[:, j * N:(j + 1) * N], in0=src[:, j, i * N:(i + 1) * N],
+                                        scalar1=decay_col[:, col:col + 1], scalar2=None, op0=ALU.mult)
+            damped[key] = dst
+
+        def weave(key, half):
+            copy = nc.scalar.copy if (key[1], key[2], half) in ACT_WEAVES else nc.vector.tensor_copy
+            if half == 0:
+                new_woven(key)
+            blocks = slice(half * N // 8, (half + 1) * N // 8)
+            copy(out=woven[key][:].rearrange("p (c i j) -> p c j i", i=4, j=PACK)[:, blocks],
+                 in_=damped[key][:].rearrange("p (j c i) -> p c j i", j=PACK, i=4)[:, blocks])
+
+        def multiply(n, h, c, g):
+            m = SLABS * h + c
+            if (n, m) not in sums:
+                sums[n, m] = take_bank()
+            b, bank = sums[n, m]
+            done[n, m] = done.get((n, m), 0) + 1
+            sta = ("weights", h, g)
+            mov = ("frames" if g < BANK_PASSES else "echo", n, g)
+            nc.tensor.matmul_mx(
+                out=bank[:],
+                lhsT=codes[sta][:, c * P:(c + 1) * P].bitcast(E4M3X4),
+                lhsT_scale=scales[sta][:, c * P:(c + 1) * P],
+                rhs=codes[mov][:].bitcast(E4M3X4 if g < BANK_PASSES else E5M2X4),
+                rhs_scale=scales[mov][:],
+                start=(done[n, m] == 1),
+                stop=(done[n, m] == PASSES),
+            )
+            if done[n, m] == PASSES:
+                result = work.tile([P, N], F32, name="result", tag="result", bufs=12, align_bytes=64)
+                pieces = 2 if (n, m) == (T // N - 1, BAND_TILES - 1) else 1
+                for i in range(pieces):
+                    lo, hi = i * N // pieces, (i + 1) * N // pieces
+                    nc.scalar.activation(out=result[:, lo:hi], in_=bank[:, lo:hi], func=ACT.Relu, bias=bias_col[:, m:m + 1])
+                    rectified.append((n, m, result, lo, hi))
+                free_banks.append(b)
+
+        def finish(count):
+            for n, m, result, lo, hi in rectified[:count]:
+                nc.vector.tensor_tensor(out=result[:, lo:hi], in0=result[:, lo:hi],
+                                        in1=gain_rows[:, n * N + lo:n * N + hi], op=ALU.mult)
+                nc.sync.dma_start(out=out_rows[:, m, n * N + lo:n * N + hi], in_=result[:, lo:hi])
+                rectified.pop(0)
+
+        identity = keep.tile([P, P], F32, name="identity", align_bytes=64)
+        make_identity(nc, identity[:])
+        bias_raw = keep.tile([P, BAND_TILES], BF16, name="bias_raw")
+        decay_raw = keep.tile([P, MIX_PASSES * PACK], BF16, name="decay_raw")
+        bias_col = keep.tile([P, BAND_TILES], F32, name="bias_col")
+        decay_col = keep.tile([P, MIX_PASSES * PACK], F32, name="decay_col")
+        gain_rows = keep.tile([P, T], BF16, name="gain_rows", align_bytes=64)
+
+        nc.scalar.dma_start(out=bias_raw[:], in_=bias.rearrange("(p m) -> p m", m=BAND_TILES))
+        nc.scalar.dma_start(out=decay_raw[:].rearrange("p (e j) -> p e j", j=PACK),
+                            in_=decay.rearrange("(e p j) -> p e j", p=P, j=PACK))
+        nc.scalar.activation(out=bias_col[:], in_=bias_raw[:], func=ACT.Identity)
+        nc.scalar.activation(out=decay_col[:], in_=decay_raw[:], func=ACT.Identity)
+        for g in range(BANK_PASSES):
+            load_frames(0, g, 1)
+            load_weights(0, g, 1)
+            if g == ECHO_AFTER:
+                load_echo(0, 4, 1)
+        load_weights(0, 4, 2)
+        load_echo(0, 5, 1)
+        load_weights(1, 0, 2)
+        load_weights(1, 2, 2)
+        load_weights(1, 4, 2)
+
+        F, W, E = "frames", "weights", "echo"
+        every = list(range(PASSES))
+        steps = [
+            ([(F, 0, 0), (W, 0, 0)], [], None, None),
+            ([(F, 0, 1), (W, 0, 1)], [(0, 0, [0])], None, None),
+            ([(F, 0, 2), (W, 0, 2)], [(0, 0, [1])], None, None),
+            ([(F, 0, 3), (W, 0, 3)], [(0, 0, [2])], (E, 0, 4), None),
+            ([(W, 0, 4), (W, 0, 5)], [(0, 0, [3])], (E, 0, 5), (E, 0, 4)),
+            ([(W, 1, 0), (W, 1, 1)], [(0, 0, [4]), (0, 0, [5])], None, (E, 0, 5)),
+            ([(W, 1, 2), (W, 1, 3)], [(0, 1, [0, 1])], (E, 1, 4), None),
+            ([(W, 1, 4), (W, 1, 5)], [(0, 1, [2, 3])], None, (E, 1, 4)),
+            ([(F, 1, 0), (F, 1, 1)], [(0, 1, [4, 5])], (E, 1, 5), None),
+            ([(F, 1, 2), (F, 1, 3)], [(1, 0, [0, 1])], None, (E, 1, 5)),
+            ([], [(1, 0, [4, 5, 2, 3])], (E, 2, 4), None),
+            ([(F, 2, 0), (F, 2, 1)], [(1, 1, every)], (E, 2, 5), (E, 2, 4)),
+            ([(F, 2, 2), (F, 2, 3)], [(2, 0, [0, 1])], None, (E, 2, 5)),
+            ([], [(2, 0, [4, 5, 2, 3]), (2, 1, every)], None, None),
+        ]
+        for s, (turned, products, begun, ended) in enumerate(steps):
+            ahead = steps[s + 1][0] if s + 1 < len(steps) else []
+            ahead = [key for key in ahead if s + 1 >= FIRST_SORTED_STEP or key in SORT_EARLY]
+            for key in turned:
+                turn(key, split=s < 2)
+            if ended:
+                weave(ended, 1)
+            for key in ahead[:1]:
+                sort_words(key)
+            if ended:
+                quantize(ended)
+            for key in ahead[1:]:
+                sort_words(key)
+            if begun:
+                damp(begun)
+            for key in turned[:1]:
+                quantize(key)
+            if begun:
+                weave(begun, 0)
+            for key in turned[1:]:
+                quantize(key)
+            if s == 1:
+                load_echo(1, 4, 1)
+                load_frames(1, 0, 2)
+                load_echo(1, 5, 1)
+                load_frames(1, 2, 2)
+                nc.sync.dma_start(out=gain_rows[:], in_=gain.partition_broadcast(P))
+                load_frames(2, 0, 2)
+                load_echo(2, 4, 1)
+                load_frames(2, 2, 2)
+                load_echo(2, 5, 1)
+            for n, h, passes in products:
+                for c in range(SLABS):
+                    if s >= FIRST_GAIN_STEP:
+                        finish(GAINS_PER_SLOT if s < 13 else LATE_GAINS)
+                    for g in passes:
+                        multiply(n, h, c, g)
+        finish(len(rectified))

@@ -25,13 +25,15 @@ BANK_PASSES = L // K_PASS
 MIX_PASSES = D // K_PASS
 PASSES = BANK_PASSES + MIX_PASSES
 BANKS = 8
-FIRST_SORTED_STEP = 6
-FIRST_GAIN_STEP = 10
-GAINS_PER_SLOT = 1
-ACT_WEAVES = ()
-SORT_EARLY = ()
-LATE_GAINS = 2
-ECHO_AFTER = 3
+ACT_WEAVES = ((0, 4, 1), (0, 5, 1))
+WARM_FIRST = 16
+WARM_NEXT = 8
+WARM_STEPS = 3
+PLAN = 0
+VAR = 2
+G11 = 1
+GAIN_FROM = 16
+UNSORTED = ()
 
 
 def tile_filter_bank_mixer_s2_kernel(tc, frames, filters, echo, decay, mixer, bias, gain, out):
@@ -62,9 +64,9 @@ def tile_filter_bank_mixer_s2_kernel(tc, frames, filters, echo, decay, mixer, bi
         def load(src, keys):
             width = len(keys) * K_PASS
             if len(keys) == 1:
-                tile = work.tile([P, SLABS * width], BF16, name="single", tag="single", bufs=10, align_bytes=64)
+                tile = work.tile([P, SLABS * width], BF16, name="single", tag="single", bufs=14, align_bytes=64)
             else:
-                tile = work.tile([P, SLABS * width], BF16, name="double", tag="double", bufs=8, align_bytes=64)
+                tile = work.tile([P, SLABS * width], BF16, name="double", tag="double", bufs=5, align_bytes=64)
             nc.sync.dma_start(out=tile[:].rearrange("p (c k) -> p c k", c=SLABS), in_=src)
             for i, key in enumerate(keys):
                 raw[key] = (tile, i, len(keys))
@@ -169,10 +171,20 @@ def tile_filter_bank_mixer_s2_kernel(tc, frames, filters, echo, decay, mixer, bi
                     rectified.append((n, m, result, lo, hi))
                 free_banks.append(b)
 
+        def warm(count):
+            b, bank = take_bank()
+            for i in range(count):
+                nc.tensor.matmul_mx(out=bank[:, :P], lhsT=zero_codes[:].bitcast(E4M3X4), lhsT_scale=zero_scales[:],
+                                    rhs=zero_codes[:].bitcast(E4M3X4), rhs_scale=zero_scales[:], start=True, stop=True)
+            free_banks.append(b)
+
+        def load_gain(n):
+            nc.sync.dma_start(out=gain_rows[n][:], in_=gain[n * N:(n + 1) * N].partition_broadcast(P))
+
         def finish(count):
             for n, m, result, lo, hi in rectified[:count]:
                 nc.vector.tensor_tensor(out=result[:, lo:hi], in0=result[:, lo:hi],
-                                        in1=gain_rows[:, n * N + lo:n * N + hi], op=ALU.mult)
+                                        in1=gain_rows[n][:, lo:hi], op=ALU.mult)
                 nc.sync.dma_start(out=out_rows[:, m, n * N + lo:n * N + hi], in_=result[:, lo:hi])
                 rectified.pop(0)
 
@@ -182,7 +194,14 @@ def tile_filter_bank_mixer_s2_kernel(tc, frames, filters, echo, decay, mixer, bi
         decay_raw = keep.tile([P, MIX_PASSES * PACK], BF16, name="decay_raw")
         bias_col = keep.tile([P, BAND_TILES], F32, name="bias_col")
         decay_col = keep.tile([P, MIX_PASSES * PACK], F32, name="decay_col")
-        gain_rows = keep.tile([P, T], BF16, name="gain_rows", align_bytes=64)
+        gain_rows = [keep.tile([P, N], BF16, name="gain_rows%d" % n, align_bytes=64) for n in range(T // N)]
+        zeros = keep.tile([P, K_PASS], BF16, name="zeros", align_bytes=64)
+        zero_codes = keep.tile([P, P], U32, name="zero_codes", align_bytes=64)
+        zero_scales = keep.tile([P, P], U8, name="zero_scales", align_bytes=64)
+        if WARM_FIRST:
+            nc.vector.memset(zeros[:], 0.0)
+            nc.vector.quantize_mx(out=zero_codes[:].bitcast(E4M3X4), scales=zero_scales[:], in_=zeros[:])
+            warm(WARM_FIRST)
 
         nc.scalar.dma_start(out=bias_raw[:], in_=bias.rearrange("(p m) -> p m", m=BAND_TILES))
         nc.scalar.dma_start(out=decay_raw[:].rearrange("p (e j) -> p e j", j=PACK),
@@ -192,37 +211,103 @@ def tile_filter_bank_mixer_s2_kernel(tc, frames, filters, echo, decay, mixer, bi
         for g in range(BANK_PASSES):
             load_frames(0, g, 1)
             load_weights(0, g, 1)
-            if g == ECHO_AFTER:
-                load_echo(0, 4, 1)
-        load_weights(0, 4, 2)
-        load_echo(0, 5, 1)
-        load_weights(1, 0, 2)
+        for g in range(BANK_PASSES, PASSES):
+            load_echo(0, g, 1)
+            load_weights(0, g, 1)
+        load_weights(1, 0, 1)
+        load_weights(1, 1, 1)
         load_weights(1, 2, 2)
         load_weights(1, 4, 2)
 
         F, W, E = "frames", "weights", "echo"
         every = list(range(PASSES))
-        steps = [
-            ([(F, 0, 0), (W, 0, 0)], [], None, None),
-            ([(F, 0, 1), (W, 0, 1)], [(0, 0, [0])], None, None),
-            ([(F, 0, 2), (W, 0, 2)], [(0, 0, [1])], None, None),
-            ([(F, 0, 3), (W, 0, 3)], [(0, 0, [2])], (E, 0, 4), None),
-            ([(W, 0, 4), (W, 0, 5)], [(0, 0, [3])], (E, 0, 5), (E, 0, 4)),
-            ([(W, 1, 0), (W, 1, 1)], [(0, 0, [4]), (0, 0, [5])], None, (E, 0, 5)),
-            ([(W, 1, 2), (W, 1, 3)], [(0, 1, [0, 1])], (E, 1, 4), None),
-            ([(W, 1, 4), (W, 1, 5)], [(0, 1, [2, 3])], None, (E, 1, 4)),
-            ([(F, 1, 0), (F, 1, 1)], [(0, 1, [4, 5])], (E, 1, 5), None),
-            ([(F, 1, 2), (F, 1, 3)], [(1, 0, [0, 1])], None, (E, 1, 5)),
-            ([], [(1, 0, [4, 5, 2, 3])], (E, 2, 4), None),
-            ([(F, 2, 0), (F, 2, 1)], [(1, 1, every)], (E, 2, 5), (E, 2, 4)),
-            ([(F, 2, 2), (F, 2, 3)], [(2, 0, [0, 1])], None, (E, 2, 5)),
-            ([], [(2, 0, [4, 5, 2, 3]), (2, 1, every)], None, None),
+        tiles = list(range(SLABS))
+
+        def products(n, h, passes, some=tiles, gains=0):
+            for c in some:
+                finish(gains)
+                for g in passes:
+                    multiply(n, h, c, g)
+
+        first = [(side, 0, g) for g in range(BANK_PASSES) for side in (F, W)]
+        for i, key in enumerate(first):
+            if i + 1 < len(first) and i + 1 not in UNSORTED:
+                sort_words(first[i + 1])
+            if i > 0:
+                quantize(first[i - 1])
+            turn(key)
+            if i < 3:
+                if i < WARM_STEPS:
+                    warm(WARM_NEXT)
+            else:
+                g, part = divmod(i - 3, 2)
+                products(0, 0, [g], tiles[2 * part:2 * part + 2])
+        load_echo(1, 4, 1)
+        load_frames(1, 0, 2)
+        load_echo(1, 5, 1)
+        load_frames(1, 2, 2)
+        load_frames(2, 0, 2)
+        load_gain(0)
+        load_echo(2, 4, 1)
+        products(0, 0, [2], tiles[2:])
+        damp((E, 0, 4))
+        quantize(first[-1])
+        weave((E, 0, 4), 0)
+        weave((E, 0, 4), 1)
+        turn((W, 0, 4))
+        products(0, 0, [3])
+        quantize((E, 0, 4))
+        damp((E, 0, 5))
+        quantize((W, 0, 4))
+        weave((E, 0, 5), 0)
+        weave((E, 0, 5), 1)
+        turn((W, 0, 5))
+        products(0, 0, [4], tiles[:2] if VAR == 2 else tiles)
+        if VAR == 0:
+            sort_words((W, 1, 0))
+            quantize((E, 0, 5))
+            sort_words((W, 1, 1))
+            quantize((W, 0, 5))
+        if VAR == 1:
+            quantize((W, 0, 5))
+            quantize((E, 0, 5))
+            sort_words((W, 1, 1))
+        if VAR == 2:
+            sort_words((W, 1, 0))
+            quantize((E, 0, 5))
+            sort_words((W, 1, 1))
+            quantize((W, 0, 5))
+            turn((W, 1, 0))
+            products(0, 0, [4], tiles[2:])
+        if PLAN == 0:
+            steps = [
+                ([(W, 1, 0), (W, 1, 1)], [(0, 0, [5], tiles, 0)], None, None),
+                ([(W, 1, 2), (W, 1, 3)], [(0, 1, [0, 1], tiles, 0)], (E, 1, 4), None),
+                ([(W, 1, 4), (W, 1, 5)], [(0, 1, [2, 3], tiles, 0)], None, (E, 1, 4)),
+                ([(F, 1, 0), (F, 1, 1)], [(0, 1, [4, 5], tiles, 0)], (E, 1, 5), None),
+                ([(F, 1, 2), (F, 1, 3)], [(1, 0, [0, 1], tiles, 0)], None, (E, 1, 5)),
+            ]
+        else:
+            steps = [
+                ([(W, 1, 0)], [(0, 0, [5], tiles, 0)], None, None),
+                ([(W, 1, 1), (W, 1, 2)], [(0, 1, [0], tiles, 0)], None, None),
+                ([(W, 1, 3), (W, 1, 4)], [(0, 1, [1, 2], tiles, 0)], (E, 1, 4), None),
+                ([(W, 1, 5), (F, 1, 0)], [(0, 1, [3, 4], tiles, 0)], None, (E, 1, 4)),
+                ([(F, 1, 1)], [(0, 1, [5], tiles, 0)], (E, 1, 5), None),
+                ([(F, 1, 2), (F, 1, 3)], [(1, 0, [0, 1], tiles, 0)], None, (E, 1, 5)),
+            ]
+        steps += [
+            ([], [(1, 0, [4, 5, 2, 3], tiles, 1)], (E, 2, 4), None),
+            ([(F, 2, 0), (F, 2, 1)], [(1, 1, every, tiles, G11)], (E, 2, 5), (E, 2, 4)),
+            ([(F, 2, 2), (F, 2, 3)], [(2, 0, [0, 1], tiles, 1)], None, (E, 2, 5)),
+            ([], [(2, 0, [4, 5, 2, 3], tiles, 2), (2, 1, every, tiles, 2)], None, None),
         ]
-        for s, (turned, products, begun, ended) in enumerate(steps):
+        for s, (turned, work_list, begun, ended) in enumerate(steps):
             ahead = steps[s + 1][0] if s + 1 < len(steps) else []
-            ahead = [key for key in ahead if s + 1 >= FIRST_SORTED_STEP or key in SORT_EARLY]
+            ahead = [key for key in ahead if key not in sorted_words]
             for key in turned:
-                turn(key, split=s < 2)
+                if key not in woven:
+                    turn(key)
             if ended:
                 weave(ended, 1)
             for key in ahead[:1]:
@@ -239,20 +324,11 @@ def tile_filter_bank_mixer_s2_kernel(tc, frames, filters, echo, decay, mixer, bi
                 weave(begun, 0)
             for key in turned[1:]:
                 quantize(key)
-            if s == 1:
-                load_echo(1, 4, 1)
-                load_frames(1, 0, 2)
-                load_echo(1, 5, 1)
-                load_frames(1, 2, 2)
-                nc.sync.dma_start(out=gain_rows[:], in_=gain.partition_broadcast(P))
-                load_frames(2, 0, 2)
-                load_echo(2, 4, 1)
+            if s == 2:
                 load_frames(2, 2, 2)
                 load_echo(2, 5, 1)
-            for n, h, passes in products:
-                for c in range(SLABS):
-                    if s >= FIRST_GAIN_STEP:
-                        finish(GAINS_PER_SLOT if s < 13 else LATE_GAINS)
-                    for g in passes:
-                        multiply(n, h, c, g)
+                load_gain(1)
+                load_gain(2)
+            for product in work_list:
+                products(*product)
         finish(len(rectified))

from contextlib import ExitStack

import concourse.mybir as mybir
from concourse.masks import make_identity

T, L, D = 1536, 2048, 1024
FLOPS = 2 * D * T * (L + D)

F32 = mybir.dt.float32
BF16 = mybir.dt.bfloat16
U32 = mybir.dt.uint32
U8 = mybir.dt.uint8
E4M3X4 = mybir.dt.float8_e4m3fn_x4
E5M2X4 = mybir.dt.float8_e5m2_x4
ACT = mybir.ActivationFunctionType
ALU = mybir.AluOpType

P = 128
PACK = 4
K_PASS = P * PACK
N = 512
SLABS = 4
BAND_TILES = D // P
BANK_PASSES = L // K_PASS
MIX_PASSES = D // K_PASS
PASSES = BANK_PASSES + MIX_PASSES
BANKS = 8
ACT_WEAVES = ((0, 4, 1), (0, 5, 1))
WARM_FIRST = 16
WARM_NEXT = 8
WARM_STEPS = 3
PLAN = 0
VAR = 2
G11 = 1
GAIN_FROM = 16
UNSORTED = ()


def tile_filter_bank_mixer_s2_kernel(tc, frames, filters, echo, decay, mixer, bias, gain, out):
    nc = tc.nc
    filter_rows = filters.rearrange("(p m) k -> p m k", m=BAND_TILES)
    mixer_rows = mixer.rearrange("(p m) k -> p m k", m=BAND_TILES)
    out_rows = out.rearrange("(p m) t -> p m t", m=BAND_TILES)
    frame_rows = frames.rearrange("(n c p) k -> n p c k", c=SLABS, p=P)
    echo_rows = echo.rearrange("(e p j) t -> e p j t", p=P, j=PACK)

    with ExitStack() as ctx:
        keep = ctx.enter_context(tc.tile_pool(name="keep", bufs=1))
        work = ctx.enter_context(tc.tile_pool(name="work", bufs=1))
        psum = ctx.enter_context(tc.psum_pool(name="psum", bufs=1))
        ctx.enter_context(tc.manual_schedule())

        raw = {}
        sorted_words = {}
        woven = {}
        damped = {}
        codes = {}
        scales = {}
        sums = {}
        done = {}
        rectified = []
        free_banks = list(range(BANKS))

        def load(src, keys):
            width = len(keys) * K_PASS
            if len(keys) == 1:
                tile = work.tile([P, SLABS * width], BF16, name="single", tag="single", bufs=14, align_bytes=64)
            else:
                tile = work.tile([P, SLABS * width], BF16, name="double", tag="double", bufs=5, align_bytes=64)
            nc.sync.dma_start(out=tile[:].rearrange("p (c k) -> p c k", c=SLABS), in_=src)
            for i, key in enumerate(keys):
                raw[key] = (tile, i, len(keys))

        def load_frames(n, g, count):
            load(frame_rows[n][:, :, g * K_PASS:(g + count) * K_PASS], [("frames", n, g + i) for i in range(count)])

        def load_weights(h, g, count):
            rows, g0 = (filter_rows, g) if g < BANK_PASSES else (mixer_rows, g - BANK_PASSES)
            load(rows[:, SLABS * h:SLABS * (h + 1), g0 * K_PASS:(g0 + count) * K_PASS],
                 [("weights", h, g + i) for i in range(count)])

        def load_echo(n, g, count):
            load(echo_rows[g - BANK_PASSES][:, :, n * N:(n + count) * N], [("echo", n + i, g) for i in range(count)])

        def raw_words(key):
            tile, i, count = raw[key]
            half = K_PASS // 2
            return tile[:].bitcast(F32).rearrange("p (c w) -> p c w", c=SLABS)[:, :, i * half:(i + 1) * half]

        def take_bank():
            b = free_banks.pop(0)
            bank = psum.tile([P, N], F32, name="bank%d" % b, tag="bank%d" % b)
            return b, bank

        def sort_words(key):
            tile = work.tile([P, SLABS * 2 * P], F32, name="sorted", tag="sorted", bufs=3, align_bytes=64)
            nc.vector.tensor_copy(out=tile[:].rearrange("p (c u w) -> p c u w", c=SLABS, u=2),
                                  in_=raw_words(key).rearrange("p c (w u) -> p c u w", u=2))
            sorted_words[key] = tile

        def new_woven(key):
            tile = work.tile([P, N * PACK], BF16, name="woven", tag="woven", bufs=5, align_bytes=64)
            woven[key] = tile
            return tile

        def turn(key, split=False):
            if key in sorted_words:
                src = sorted_words[key][:].rearrange("p (c u w) -> p c u w", c=SLABS, u=2)
            else:
                src = raw_words(key).rearrange("p c (w u) -> p c u w", u=2)
            dst = new_woven(key)[:].bitcast(F32)
            for pair in range(SLABS // 2):
                b, bank = take_bank()
                for c in range(2):
                    for u in range(2):
                        j = 2 * c + u
                        nc.tensor.transpose(bank[:, j * P:(j + 1) * P], src[:, 2 * pair + c, u, :], identity[:])
                copy = nc.vector.tensor_copy if split and pair == 1 else nc.scalar.copy
                copy(out=dst[:, pair * N:(pair + 1) * N].rearrange("p (c r u) -> p c r u", c=2, u=2),
                     in_=bank[:].rearrange("p (c u r) -> p c r u", c=2, u=2))
                free_banks.append(b)

        def quantize(key):
            side = "stationary" if key[0] == "weights" else "moving"
            codes[key] = keep.tile([P, N], U32, name="codes_%s%d%d" % key, tag="codes_" + side, bufs=2 * PASSES, align_bytes=64)
            scales[key] = keep.tile([P, N], U8, name="scales_%s%d%d" % key, tag="scales_" + side, bufs=2 * PASSES, align_bytes=64)
            fmt = E5M2X4 if key[0] == "echo" else E4M3X4
            nc.vector.quantize_mx(out=codes[key][:].bitcast(fmt), scales=scales[key][:], in_=woven[key][:])

        def damp(key):
            tile, i, count = raw[key]
            src = tile[:].rearrange("p (j t) -> p j t", j=PACK)
            dst = work.tile([P, PACK * N], BF16, name="damped", tag="damped", bufs=2, align_bytes=64)
            for j in range(PACK):
                col = (key[2] - BANK_PASSES) * PACK + j
                nc.vector.tensor_scalar(out=dst[:, j * N:(j + 1) * N], in0=src[:, j, i * N:(i + 1) * N],
                                        scalar1=decay_col[:, col:col + 1], scalar2=None, op0=ALU.mult)
            damped[key] = dst

        def weave(key, half):
            copy = nc.scalar.copy if (key[1], key[2], half) in ACT_WEAVES else nc.vector.tensor_copy
            if half == 0:
                new_woven(key)
            blocks = slice(half * N // 8, (half + 1) * N // 8)
            copy(out=woven[key][:].rearrange("p (c i j) -> p c j i", i=4, j=PACK)[:, blocks],
                 in_=damped[key][:].rearrange("p (j c i) -> p c j i", j=PACK, i=4)[:, blocks])

        def multiply(n, h, c, g):
            m = SLABS * h + c
            if (n, m) not in sums:
                sums[n, m] = take_bank()
            b, bank = sums[n, m]
            done[n, m] = done.get((n, m), 0) + 1
            sta = ("weights", h, g)
            mov = ("frames" if g < BANK_PASSES else "echo", n, g)
            nc.tensor.matmul_mx(
                out=bank[:],
                lhsT=codes[sta][:, c * P:(c + 1) * P].bitcast(E4M3X4),
                lhsT_scale=scales[sta][:, c * P:(c + 1) * P],
                rhs=codes[mov][:].bitcast(E4M3X4 if g < BANK_PASSES else E5M2X4),
                rhs_scale=scales[mov][:],
                start=(done[n, m] == 1),
                stop=(done[n, m] == PASSES),
            )
            if done[n, m] == PASSES:
                result = work.tile([P, N], F32, name="result", tag="result", bufs=12, align_bytes=64)
                pieces = 2 if (n, m) == (T // N - 1, BAND_TILES - 1) else 1
                for i in range(pieces):
                    lo, hi = i * N // pieces, (i + 1) * N // pieces
                    nc.scalar.activation(out=result[:, lo:hi], in_=bank[:, lo:hi], func=ACT.Relu, bias=bias_col[:, m:m + 1])
                    rectified.append((n, m, result, lo, hi))
                free_banks.append(b)

        def warm(count):
            b, bank = take_bank()
            for i in range(count):
                nc.tensor.matmul_mx(out=bank[:, :P], lhsT=zero_codes[:].bitcast(E4M3X4), lhsT_scale=zero_scales[:],
                                    rhs=zero_codes[:].bitcast(E4M3X4), rhs_scale=zero_scales[:], start=True, stop=True)
            free_banks.append(b)

        def load_gain(n):
            nc.sync.dma_start(out=gain_rows[n][:], in_=gain[n * N:(n + 1) * N].partition_broadcast(P))

        def finish(count):
            for n, m, result, lo, hi in rectified[:count]:
                nc.vector.tensor_tensor(out=result[:, lo:hi], in0=result[:, lo:hi],
                                        in1=gain_rows[n][:, lo:hi], op=ALU.mult)
                nc.sync.dma_start(out=out_rows[:, m, n * N + lo:n * N + hi], in_=result[:, lo:hi])
                rectified.pop(0)

        identity = keep.tile([P, P], F32, name="identity", align_bytes=64)
        make_identity(nc, identity[:])
        bias_raw = keep.tile([P, BAND_TILES], BF16, name="bias_raw")
        decay_raw = keep.tile([P, MIX_PASSES * PACK], BF16, name="decay_raw")
        bias_col = keep.tile([P, BAND_TILES], F32, name="bias_col")
        decay_col = keep.tile([P, MIX_PASSES * PACK], F32, name="decay_col")
        gain_rows = [keep.tile([P, N], BF16, name="gain_rows%d" % n, align_bytes=64) for n in range(T // N)]
        zeros = keep.tile([P, K_PASS], BF16, name="zeros", align_bytes=64)
        zero_codes = keep.tile([P, P], U32, name="zero_codes", align_bytes=64)
        zero_scales = keep.tile([P, P], U8, name="zero_scales", align_bytes=64)
        if WARM_FIRST:
            nc.vector.memset(zeros[:], 0.0)
            nc.vector.quantize_mx(out=zero_codes[:].bitcast(E4M3X4), scales=zero_scales[:], in_=zeros[:])
            warm(WARM_FIRST)

        nc.scalar.dma_start(out=bias_raw[:], in_=bias.rearrange("(p m) -> p m", m=BAND_TILES))
        nc.scalar.dma_start(out=decay_raw[:].rearrange("p (e j) -> p e j", j=PACK),
                            in_=decay.rearrange("(e p j) -> p e j", p=P, j=PACK))
        nc.scalar.activation(out=bias_col[:], in_=bias_raw[:], func=ACT.Identity)
        nc.scalar.activation(out=decay_col[:], in_=decay_raw[:], func=ACT.Identity)
        for g in range(BANK_PASSES):
            load_frames(0, g, 1)
            load_weights(0, g, 1)
        for g in range(BANK_PASSES, PASSES):
            load_echo(0, g, 1)
            load_weights(0, g, 1)
        load_weights(1, 0, 1)
        load_weights(1, 1, 1)
        load_weights(1, 2, 2)
        load_weights(1, 4, 2)

        F, W, E = "frames", "weights", "echo"
        every = list(range(PASSES))
        tiles = list(range(SLABS))

        def products(n, h, passes, some=tiles, gains=0):
            for c in some:
                finish(gains)
                for g in passes:
                    multiply(n, h, c, g)

        first = [(side, 0, g) for g in range(BANK_PASSES) for side in (F, W)]
        for i, key in enumerate(first):
            if i + 1 < len(first) and i + 1 not in UNSORTED:
                sort_words(first[i + 1])
            if i > 0:
                quantize(first[i - 1])
            turn(key)
            if i < 3:
                if i < WARM_STEPS:
                    warm(WARM_NEXT)
            else:
                g, part = divmod(i - 3, 2)
                products(0, 0, [g], tiles[2 * part:2 * part + 2])
        load_echo(1, 4, 1)
        load_frames(1, 0, 2)
        load_echo(1, 5, 1)
        load_frames(1, 2, 2)
        load_frames(2, 0, 2)
        load_gain(0)
        load_echo(2, 4, 1)
        products(0, 0, [2], tiles[2:])
        damp((E, 0, 4))
        quantize(first[-1])
        weave((E, 0, 4), 0)
        weave((E, 0, 4), 1)
        turn((W, 0, 4))
        products(0, 0, [3])
        quantize((E, 0, 4))
        damp((E, 0, 5))
        quantize((W, 0, 4))
        weave((E, 0, 5), 0)
        weave((E, 0, 5), 1)
        turn((W, 0, 5))
        products(0, 0, [4], tiles[:2] if VAR == 2 else tiles)
        if VAR == 0:
            sort_words((W, 1, 0))
            quantize((E, 0, 5))
            sort_words((W, 1, 1))
            quantize((W, 0, 5))
        if VAR == 1:
            quantize((W, 0, 5))
            quantize((E, 0, 5))
            sort_words((W, 1, 1))
        if VAR == 2:
            sort_words((W, 1, 0))
            quantize((E, 0, 5))
            sort_words((W, 1, 1))
            quantize((W, 0, 5))
            turn((W, 1, 0))
            products(0, 0, [4], tiles[2:])
        if PLAN == 0:
            steps = [
                ([(W, 1, 0), (W, 1, 1)], [(0, 0, [5], tiles, 0)], None, None),
                ([(W, 1, 2), (W, 1, 3)], [(0, 1, [0, 1], tiles, 0)], (E, 1, 4), None),
                ([(W, 1, 4), (W, 1, 5)], [(0, 1, [2, 3], tiles, 0)], None, (E, 1, 4)),
                ([(F, 1, 0), (F, 1, 1)], [(0, 1, [4, 5], tiles, 0)], (E, 1, 5), None),
                ([(F, 1, 2), (F, 1, 3)], [(1, 0, [0, 1], tiles, 0)], None, (E, 1, 5)),
            ]
        else:
            steps = [
                ([(W, 1, 0)], [(0, 0, [5], tiles, 0)], None, None),
                ([(W, 1, 1), (W, 1, 2)], [(0, 1, [0], tiles, 0)], None, None),
                ([(W, 1, 3), (W, 1, 4)], [(0, 1, [1, 2], tiles, 0)], (E, 1, 4), None),
                ([(W, 1, 5), (F, 1, 0)], [(0, 1, [3, 4], tiles, 0)], None, (E, 1, 4)),
                ([(F, 1, 1)], [(0, 1, [5], tiles, 0)], (E, 1, 5), None),
                ([(F, 1, 2), (F, 1, 3)], [(1, 0, [0, 1], tiles, 0)], None, (E, 1, 5)),
            ]
        steps += [
            ([], [(1, 0, [4, 5, 2, 3], tiles, 1)], (E, 2, 4), None),
            ([(F, 2, 0), (F, 2, 1)], [(1, 1, every, tiles, G11)], (E, 2, 5), (E, 2, 4)),
            ([(F, 2, 2), (F, 2, 3)], [(2, 0, [0, 1], tiles, 1)], None, (E, 2, 5)),
            ([], [(2, 0, [4, 5, 2, 3], tiles, 2), (2, 1, every, tiles, 2)], None, None),
        ]
        for s, (turned, work_list, begun, ended) in enumerate(steps):
            ahead = steps[s + 1][0] if s + 1 < len(steps) else []
            ahead = [key for key in ahead if key not in sorted_words]
            for key in turned:
                if key not in woven:
                    turn(key)
            if ended:
                weave(ended, 1)
            for key in ahead[:1]:
                sort_words(key)
            if ended:
                quantize(ended)
            for key in ahead[1:]:
                sort_words(key)
            if begun:
                damp(begun)
            for key in turned[:1]:
                quantize(key)
            if begun:
                weave(begun, 0)
            for key in turned[1:]:
                quantize(key)
            if s == 2:
                load_frames(2, 2, 2)
                load_echo(2, 5, 1)
                load_gain(1)
                load_gain(2)
            for product in work_list:
                products(*product)
        finish(len(rectified))
